import numpy as np
import ml_dtypes


def mxq(x, axis, fmt="e4m3"):
    dtype, down = {"e4m3": (ml_dtypes.float8_e4m3fn, 7), "e5m2": (ml_dtypes.float8_e5m2, 14)}[fmt]
    v = np.moveaxis(np.asarray(x, np.float32).astype(ml_dtypes.bfloat16).astype(np.float64), axis, -1)
    blocks = v.reshape(v.shape[:-1] + (-1, 32))
    amax = np.abs(blocks).max(-1, keepdims=True)
    byte = np.maximum(np.where(amax > 0, np.frexp(amax)[1] - 1 + 127, 0) - down, 1)
    scale = np.exp2(byte - 127.0)
    codes = (blocks / scale).astype(np.float32).astype(dtype).astype(np.float64)
    return np.moveaxis((codes * scale).reshape(v.shape), -1, axis)


WIDE = False


def mx_kscale(k):
    if not WIDE:
        return np.ones(k)
    levels = np.array([30, -30])
    if k % 512:
        return np.exp2(np.random.permutation(np.resize(levels, k // 32))).repeat(32)
    a = np.empty((k // 512, 16))
    for p in range(k // 512):
        a[p, :8] = np.random.permutation(np.resize(levels, 8))
        for g in range(8):
            far = levels[np.abs(levels - a[p, g]) >= 10]
            a[p, g + 8] = far[np.random.randint(len(far))]
    return np.exp2(a.ravel()).repeat(32)


def f64(x):
    return np.asarray(x).astype(np.float64)


def striped(idx):
    return np.tile(np.asarray(idx).reshape(-1, 16).T, (8, 1)).astype(np.uint16)


def unstriped(offs):
    return offs[:16].T.reshape(-1).astype(np.int64)


def striped8(idx):
    return np.asarray(idx).reshape(8, -1, 16).transpose(0, 2, 1).reshape(128, -1).astype(np.uint16)


def unstriped8(offs):
    return offs.reshape(8, 16, -1).transpose(0, 2, 1).reshape(8, -1).astype(np.int64)


def pick8(x, idx, run):
    r = np.arange(len(x))
    return x[r[:, None], idx[r % (8 * run) // run]]


E2M1 = np.array([0.0, 0.5, 1.0, 1.5, 2.0, 3.0, 4.0, 6.0, -0.0, -0.5, -1.0, -1.5, -2.0, -3.0, -4.0, -6.0])


def pack_weight(w, fmt):
    k, n = w.shape
    w = f64(np.asarray(w, np.float32).astype(ml_dtypes.bfloat16)).reshape(k // 32, 32, n)
    amax = np.abs(w).max(1)
    if fmt in ("e4m3", "e5m2"):
        byte = np.frexp(amax)[1] - 1 + 127 - (7 if fmt == "e4m3" else 14)
    else:
        mant, ex = np.frexp(amax / 6.0)
        byte = np.where(mant > 0.5, ex, ex - 1) + 127
    byte = np.clip(np.where(amax > 0, byte, 1), 1, 254)
    scaled = (w * np.exp2(127.0 - byte)[:, None, :]).reshape(k, n).astype(np.float32)
    by_word = np.ascontiguousarray(scaled.reshape(k // 512, 128, 4, n).transpose(0, 1, 3, 2))
    if fmt in ("e4m3", "e5m2"):
        words = by_word.astype(ml_dtypes.float8_e4m3fn if fmt == "e4m3" else ml_dtypes.float8_e5m2).view(np.uint8)
    else:
        c = by_word.astype(ml_dtypes.float4_e2m1fn).view(np.uint8) & 0xF
        words = (c[..., 0::2] | (c[..., 1::2] << 4)).reshape(k // 512, 128, 2 * n)
    return np.ascontiguousarray(words), np.ascontiguousarray(byte.astype(np.uint8).reshape(k // 512, 16, n))


def unpack_weight(words, scales, fmt):
    g, _, n = scales.shape
    words = np.ascontiguousarray(words).reshape(g, 128, n, -1)
    if fmt in ("e4m3", "e5m2"):
        vals = words.view(ml_dtypes.float8_e4m3fn if fmt == "e4m3" else ml_dtypes.float8_e5m2).astype(np.float64)
    else:
        nib = np.empty((g, 128, n, 4), np.uint8)
        nib[..., 0::2] = words & 0xF
        nib[..., 1::2] = words >> 4
        vals = E2M1[nib]
    vals = vals * np.repeat(np.exp2(scales.astype(np.float64) - 127.0), 8, axis=1)[..., None]
    return vals.transpose(0, 1, 3, 2).reshape(g * 512, n)


K, T, J, R, C, O, N, E = 512, 1024, 256, 512, 512, 128, 256, 512


def setup_inputs():
    n = np.random.standard_normal
    idx = np.random.permutation(T)[:J]
    idx2 = np.stack([np.random.permutation(C)[:J] for _ in range(8)])
    idx3 = np.random.permutation(C)[:O]
    idx4 = np.random.permutation(C)[:O]
    idx5 = np.random.permutation(E)[:O]
    idx6 = np.random.permutation(E)[:O]
    fk = mx_kscale(K)
    fr = mx_kscale(R)
    xtp = pack_weight(n((K, T)) / fk[:, None], "e4m3")
    wp = pack_weight(n((K, R)) * 1 / np.sqrt(K) * fk[:, None] * fr, "e2m1")
    wbp = pack_weight(n((R, N)) * 1 / np.sqrt(R) / fr[:, None], "e5m2")
    return {
        "xt_words": xtp[0],
        "xt_scales": xtp[1],
        "w_words": wp[0],
        "w_scales": wp[1],
        "sa": (np.random.uniform(0.5, 1.6, (R, 1))).astype(np.float32),
        "sb": (np.random.uniform(0.5, 1.6, (R, 1))).astype(np.float32),
        "wb_words": wbp[0],
        "wb_scales": wbp[1],
        "offs": striped(idx),
        "offs2": striped8(idx2),
        "offs3": striped(idx3),
        "offs4": striped(idx4),
        "offs5": striped(idx5),
        "offs6": striped(idx6),
    }


def reference(xt_words, xt_scales, w_words, w_scales, sa, sb, wb_words, wb_scales, offs, offs2, offs3, offs4, offs5, offs6):
    idx = unstriped(offs)
    idx2 = unstriped8(offs2)
    idx3 = unstriped(offs3)
    idx4 = unstriped(offs4)
    idx5 = unstriped(offs5)
    idx6 = unstriped(offs6)
    xtu = unpack_weight(xt_words, xt_scales, "e4m3")
    wu = unpack_weight(w_words, w_scales, "e2m1")
    wbu = unpack_weight(wb_words, wb_scales, "e5m2")
    xtidxg = xtu[:, idx]
    a = wu.T @ xtidxg
    pw = np.zeros((R, C))
    pw[np.arange(R)[:, None], idx2[np.arange(R) % 512 // 64]] = a
    hid = np.abs(pw[:, idx3] * f64(sa) - pw[:, idx4] * f64(sb))
    hidq = mxq(hid, 0, "e4m3")
    p = wbu.T @ hidq
    pa = np.zeros((N, E))
    pa[:, idx5] = p
    pb = np.zeros((N, E))
    pb[:, idx6] = p
    y = pa + pb
    return y

@@ -1,0 +1,144 @@
+from contextlib import ExitStack
+
+import concourse.mybir as mybir
+
+K, T, J, R, C, O, N, E = 512, 1024, 256, 512, 512, 128, 256, 512
+FLOPS = 2 * K * R * J + 2 * R * N * O
+
+P = 128
+PACK = 4
+F32 = mybir.dt.float32
+BF16 = mybir.dt.bfloat16
+I32 = mybir.dt.int32
+U32 = mybir.dt.uint32
+U16 = mybir.dt.uint16
+U8 = mybir.dt.uint8
+E4M3 = mybir.dt.float8_e4m3fn_x4
+E5M2 = mybir.dt.float8_e5m2_x4
+E2M1 = mybir.dt.float4_e2m1fn_x4
+ALU = mybir.AluOpType
+COPY = mybir.ActivationFunctionType.Copy
+
+
+def tile_list_ownboard_solo_one_pagetwice_kernel(tc, xt_words, xt_scales, w_words, w_scales, sa, sb, wb_words, wb_scales,
+                                                    offs, offs2, offs3, offs4, offs5, offs6, out):
+    nc = tc.nc
+    with ExitStack() as ctx:
+        lists = ctx.enter_context(tc.tile_pool(name="lists", bufs=1))
+        pool = ctx.enter_context(tc.tile_pool(name="pool", bufs=1))
+        psum = ctx.enter_context(tc.psum_pool(name="psum", bufs=1))
+
+        def load_list(src, name):
+            t = lists.tile(list(src.shape), U16, name=name)
+            nc.sync.dma_start(out=t[:], in_=src)
+            return t
+
+        def load_plane(queue, plane, scales):
+            for q in range(4):
+                queue.dma_start(out=plane[32 * q:32 * q + 4, :].bitcast(I32), in_=scales[0, 4 * q:4 * q + 4, :].bitcast(I32))
+
+        xt_plane = pool.tile([P, T], U8, name="xt_plane", align_bytes=64)
+        w_plane = pool.tile([P, R], U8, name="w_plane", align_bytes=64)
+        wb_plane = pool.tile([P, N], U8, name="wb_plane", align_bytes=64)
+        nc.vector.memset(xt_plane[:].bitcast(I32), 0)
+        nc.vector.memset(w_plane[:].bitcast(I32), 0)
+        boards = [pool.tile([P, C], F32, name="board%d" % t, align_bytes=64) for t in range(PACK)]
+        for t in range(PACK):
+            nc.vector.memset(boards[t][:], 0.0)
+        nc.vector.memset(wb_plane[:].bitcast(I32), 0)
+
+        idx = load_list(offs, "idx")
+        xt_codes = pool.tile([P, T], U32, name="xt_codes", align_bytes=64)
+        nc.sync.dma_start(out=xt_codes[:].bitcast(I32), in_=xt_words[0].rearrange("p n t -> p (n t)").bitcast(I32))
+        load_plane(nc.scalar, xt_plane, xt_scales)
+        w_codes = pool.tile([P, R], U16, name="w_codes", align_bytes=64)
+        nc.sync.dma_start(out=w_codes[:].bitcast(I32), in_=w_words[0].bitcast(I32))
+        w_rows = pool.tile([4, 4, R // 4], I32, name="w_rows", align_bytes=64)
+        nc.sync.dma_start(out=w_rows[:], in_=w_scales[0].bitcast(I32).rearrange("(q r) c -> r q c", r=4))
+        idx2 = load_list(offs2, "idx2")
+        sa_t = pool.tile([P, PACK], F32, name="sa_t")
+        nc.sync.dma_start(out=sa_t[:], in_=sa.rearrange("(p t) o -> p (t o)", t=PACK))
+        idx3 = load_list(offs3, "idx3")
+        sb_t = pool.tile([P, PACK], F32, name="sb_t")
+        nc.sync.dma_start(out=sb_t[:], in_=sb.rearrange("(p t) o -> p (t o)", t=PACK))
+        idx4 = load_list(offs4, "idx4")
+        wb_codes = pool.tile([P, N], U32, name="wb_codes", align_bytes=64)
+        nc.sync.dma_start(out=wb_codes[:].bitcast(I32), in_=wb_words[0].rearrange("p n t -> p (n t)").bitcast(I32))
+        load_plane(nc.sync, wb_plane, wb_scales)
+        idx5 = load_list(offs5, "idx5")
+        idx6 = load_list(offs6, "idx6")
+
+        xg_plane = pool.tile([P, J], U8, name="xg_plane", align_bytes=64)
+        nc.vector.tensor_copy(out=xg_plane[:], in_=xt_plane[:].indirect(idx[:]))
+        for q in range(4):
+            nc.vector.tensor_copy(out=w_plane[32 * q:32 * q + 4, :].bitcast(I32), in_=w_rows[:, q, :])
+        xg_codes = pool.tile([P, J], U32, name="xg_codes", align_bytes=64)
+        nc.vector.tensor_copy(out=xg_codes[:], in_=xt_codes[:].indirect(idx[:]))
+
+        a_sb = []
+        for t in range(PACK):
+            wt_codes = pool.tile([P, P], U16, name="wt_codes%d" % t, align_bytes=64)
+            wt_plane = pool.tile([P, P], U8, name="wt_plane%d" % t, align_bytes=64)
+            nc.vector.tensor_copy(out=wt_codes[:], in_=w_codes[:, t:R:PACK])
+            nc.vector.tensor_copy(out=wt_plane[:], in_=w_plane[:, t:R:PACK])
+            a_ps = psum.tile([P, J], F32, name="a_ps%d" % t)
+            nc.tensor.matmul_mx(out=a_ps[:], lhsT=wt_codes[:].bitcast(E2M1), lhsT_scale=wt_plane[:],
+                                rhs=xg_codes[:].bitcast(E4M3), rhs_scale=xg_plane[:], start=True, stop=True)
+            a_t = pool.tile([P, J], F32, name="a_sb%d" % t, align_bytes=64)
+            nc.vector.tensor_copy(out=a_t[:], in_=a_ps[:])
+            a_sb.append(a_t)
+
+        first = pool.tile([P, PACK, O], F32, name="first", align_bytes=64)
+        second = pool.tile([P, PACK, O], F32, name="second", align_bytes=64)
+        diff = pool.tile([P, PACK, O], F32, name="diff", align_bytes=64)
+        hid = pool.tile([P, O, PACK], BF16, name="hid", align_bytes=64)
+
+        def put(t):
+            nc.scalar.activation(out=boards[t][:].indirect(idx2[:]), in_=a_sb[t][:], func=COPY)
+
+        def fetch(t):
+            nc.scalar.activation(out=first[:, t, :], in_=boards[t][:].indirect(idx3[:]), func=COPY, scale=sa_t[:, t:t + 1])
+            nc.scalar.activation(out=second[:, t, :], in_=boards[t][:].indirect(idx4[:]), func=COPY, scale=sb_t[:, t:t + 1])
+            nc.vector.tensor_tensor(out=diff[:, t, :], in0=first[:, t, :], in1=second[:, t, :], op=ALU.subtract)
+            if t % 2 == 1:
+                pair = diff[:, t - 1:t + 1, :].rearrange("p t o -> p o t")
+                nc.vector.scalar_tensor_tensor(out=hid[:, :, t - 1:t + 1], in0=pair, scalar=-1.0, in1=pair, op0=ALU.mult, op1=ALU.max)
+
+        put(0)
+        for t in range(1, PACK):
+            put(t)
+            fetch(t - 1)
+        fetch(PACK - 1)
+
+        hid_codes = pool.tile([P, O], U32, name="hid_codes", align_bytes=64)
+        hid_plane = pool.tile([P, O], U8, name="hid_plane", align_bytes=64)
+        nc.vector.quantize_mx(out=hid_codes[:].bitcast(E4M3), scales=hid_plane[:], in_=hid[:].rearrange("p o t -> p (o t)"))
+
+        halves = N // P
+        page_a = [pool.tile([P, E], F32, name="page_a%d" % h, tag=("a_sb0", "board0")[h], align_bytes=64) for h in range(halves)]
+        page_b = [pool.tile([P, E], F32, name="page_b%d" % h, tag=("a_sb1", "board1")[h], align_bytes=64) for h in range(halves)]
+        for h in range(halves):
+            nc.vector.memset(page_a[h][:], 0.0)
+            nc.vector.memset(page_b[h][:], 0.0)
+
+        p_sb = []
+        for h in range(halves):
+            cols = slice(h * P, (h + 1) * P)
+            p_ps = psum.tile([P, O], F32, name="p_ps%d" % h)
+            nc.tensor.matmul_mx(out=p_ps[:], lhsT=wb_codes[:, cols].bitcast(E5M2), lhsT_scale=wb_plane[:, cols],
+                                rhs=hid_codes[:].bitcast(E4M3), rhs_scale=hid_plane[:], start=True, stop=True)
+            p_h = pool.tile([P, O], F32, name="p_sb%d" % h, align_bytes=64)
+            if h == 0:
+                nc.vector.tensor_copy(out=p_h[:], in_=p_ps[:])
+            else:
+                nc.scalar.copy(out=p_h[:], in_=p_ps[:])
+            p_sb.append(p_h)
+        for h in range(halves):
+            nc.vector.tensor_copy(out=page_a[h][:].indirect(idx5[:]), in_=p_sb[h][:])
+            nc.scalar.activation(out=page_b[h][:].indirect(idx6[:]), in_=p_sb[h][:], func=COPY)
+        for h in range(halves):
+            for s in range(2):
+                cols = slice(s * E // 2, (s + 1) * E // 2)
+                total = pool.tile([P, E // 2], F32, name="total%d_%d" % (h, s), align_bytes=64)
+                nc.vector.tensor_tensor(out=total[:], in0=page_a[h][:, cols], in1=page_b[h][:, cols], op=ALU.add)
+                nc.sync.dma_start(out=out[h * P:(h + 1) * P, cols], in_=total[:])

@@ -35,7 +35,7 @@ def tile_list_ownboard_solo_one_pagetwice_kernel(tc, xt_words, xt_scales, w_word
 
         def load_plane(queue, plane, scales):
             for q in range(4):
-                queue.dma_start(out=plane[32 * q:32 * q + 4, :].bitcast(I32), in_=scales[0, 4 * q:4 * q + 4, :].bitcast(I32))
+                queue[q].dma_start(out=plane[32 * q:32 * q + 4, :].bitcast(I32), in_=scales[0, 4 * q:4 * q + 4, :].bitcast(I32))
 
         xt_plane = pool.tile([P, T], U8, name="xt_plane", align_bytes=64)
         w_plane = pool.tile([P, R], U8, name="w_plane", align_bytes=64)
@@ -44,17 +44,17 @@ def tile_list_ownboard_solo_one_pagetwice_kernel(tc, xt_words, xt_scales, w_word
         nc.vector.memset(w_plane[:].bitcast(I32), 0)
         boards = [pool.tile([P, C], F32, name="board%d" % t, align_bytes=64) for t in range(PACK)]
         for t in range(PACK):
-            nc.vector.memset(boards[t][:], 0.0)
+            (nc.vector if t == 0 else nc.gpsimd).memset(boards[t][:], 0.0)
         nc.vector.memset(wb_plane[:].bitcast(I32), 0)
 
         idx = load_list(offs, "idx")
-        xt_codes = pool.tile([P, T], U32, name="xt_codes", align_bytes=64)
-        nc.sync.dma_start(out=xt_codes[:].bitcast(I32), in_=xt_words[0].rearrange("p n t -> p (n t)").bitcast(I32))
-        load_plane(nc.scalar, xt_plane, xt_scales)
         w_codes = pool.tile([P, R], U16, name="w_codes", align_bytes=64)
         nc.sync.dma_start(out=w_codes[:].bitcast(I32), in_=w_words[0].bitcast(I32))
+        xt_codes = pool.tile([P, T], U32, name="xt_codes", align_bytes=64)
+        nc.sync.dma_start(out=xt_codes[:].bitcast(I32), in_=xt_words[0].rearrange("p n t -> p (n t)").bitcast(I32))
         w_rows = pool.tile([4, 4, R // 4], I32, name="w_rows", align_bytes=64)
-        nc.sync.dma_start(out=w_rows[:], in_=w_scales[0].bitcast(I32).rearrange("(q r) c -> r q c", r=4))
+        nc.scalar.dma_start(out=w_rows[:], in_=w_scales[0].bitcast(I32).rearrange("(q r) c -> r q c", r=4))
+        load_plane((nc.sync, nc.scalar, nc.sync, nc.scalar), xt_plane, xt_scales)
         idx2 = load_list(offs2, "idx2")
         sa_t = pool.tile([P, PACK], F32, name="sa_t")
         nc.sync.dma_start(out=sa_t[:], in_=sa.rearrange("(p t) o -> p (t o)", t=PACK))
@@ -64,62 +64,103 @@ def tile_list_ownboard_solo_one_pagetwice_kernel(tc, xt_words, xt_scales, w_word
         idx4 = load_list(offs4, "idx4")
         wb_codes = pool.tile([P, N], U32, name="wb_codes", align_bytes=64)
         nc.sync.dma_start(out=wb_codes[:].bitcast(I32), in_=wb_words[0].rearrange("p n t -> p (n t)").bitcast(I32))
-        load_plane(nc.sync, wb_plane, wb_scales)
+        load_plane([nc.sync] * 4, wb_plane, wb_scales)
         idx5 = load_list(offs5, "idx5")
         idx6 = load_list(offs6, "idx6")
 
         xg_plane = pool.tile([P, J], U8, name="xg_plane", align_bytes=64)
-        nc.vector.tensor_copy(out=xg_plane[:], in_=xt_plane[:].indirect(idx[:]))
-        for q in range(4):
-            nc.vector.tensor_copy(out=w_plane[32 * q:32 * q + 4, :].bitcast(I32), in_=w_rows[:, q, :])
         xg_codes = pool.tile([P, J], U32, name="xg_codes", align_bytes=64)
-        nc.vector.tensor_copy(out=xg_codes[:], in_=xt_codes[:].indirect(idx[:]))
-
-        a_sb = []
-        for t in range(PACK):
-            wt_codes = pool.tile([P, P], U16, name="wt_codes%d" % t, align_bytes=64)
-            wt_plane = pool.tile([P, P], U8, name="wt_plane%d" % t, align_bytes=64)
-            nc.vector.tensor_copy(out=wt_codes[:], in_=w_codes[:, t:R:PACK])
-            nc.vector.tensor_copy(out=wt_plane[:], in_=w_plane[:, t:R:PACK])
-            a_ps = psum.tile([P, J], F32, name="a_ps%d" % t)
-            nc.tensor.matmul_mx(out=a_ps[:], lhsT=wt_codes[:].bitcast(E2M1), lhsT_scale=wt_plane[:],
-                                rhs=xg_codes[:].bitcast(E4M3), rhs_scale=xg_plane[:], start=True, stop=True)
-            a_t = pool.tile([P, J], F32, name="a_sb%d" % t, align_bytes=64)
-            nc.vector.tensor_copy(out=a_t[:], in_=a_ps[:])
-            a_sb.append(a_t)
-
+        wt_codes, wt_plane = {}, {}
+        a_sb = [pool.tile([P, J], F32, name="a_sb%d" % t, align_bytes=64) for t in range(PACK)]
         first = pool.tile([P, PACK, O], F32, name="first", align_bytes=64)
         second = pool.tile([P, PACK, O], F32, name="second", align_bytes=64)
         diff = pool.tile([P, PACK, O], F32, name="diff", align_bytes=64)
         hid = pool.tile([P, O, PACK], BF16, name="hid", align_bytes=64)
-
-        def put(t):
-            nc.scalar.activation(out=boards[t][:].indirect(idx2[:]), in_=a_sb[t][:], func=COPY)
-
-        def fetch(t):
-            nc.scalar.activation(out=first[:, t, :], in_=boards[t][:].indirect(idx3[:]), func=COPY, scale=sa_t[:, t:t + 1])
-            nc.scalar.activation(out=second[:, t, :], in_=boards[t][:].indirect(idx4[:]), func=COPY, scale=sb_t[:, t:t + 1])
-            nc.vector.tensor_tensor(out=diff[:, t, :], in0=first[:, t, :], in1=second[:, t, :], op=ALU.subtract)
-            if t % 2 == 1:
-                pair = diff[:, t - 1:t + 1, :].rearrange("p t o -> p o t")
-                nc.vector.scalar_tensor_tensor(out=hid[:, :, t - 1:t + 1], in0=pair, scalar=-1.0, in1=pair, op0=ALU.mult, op1=ALU.max)
-
-        put(0)
-        for t in range(1, PACK):
-            put(t)
-            fetch(t - 1)
-        fetch(PACK - 1)
-
         hid_codes = pool.tile([P, O], U32, name="hid_codes", align_bytes=64)
         hid_plane = pool.tile([P, O], U8, name="hid_plane", align_bytes=64)
-        nc.vector.quantize_mx(out=hid_codes[:].bitcast(E4M3), scales=hid_plane[:], in_=hid[:].rearrange("p o t -> p (o t)"))
 
+        def entries(lst, cols):
+            return lst[:, cols.start // 16:cols.stop // 16]
+
+        def pick_scales(cols):
+            nc.vector.tensor_copy(out=xg_plane[:, cols], in_=xt_plane[:].indirect(entries(idx, cols)))
+
+        def deal_pair(t):
+            codes = pool.tile([P, 2, P], U16, name="wt_codes%d" % t, tag="wt_codes", align_bytes=64)
+            plane = pool.tile([P, 2, P], U8, name="wt_plane%d" % t, tag="wt_plane", align_bytes=64)
+            nc.vector.tensor_copy(out=codes[:], in_=w_codes[:].rearrange("p (m t) -> p t m", t=PACK)[:, t:t + 2, :])
+            nc.vector.tensor_copy(out=plane[:], in_=w_plane[:].rearrange("p (m t) -> p t m", t=PACK)[:, t:t + 2, :])
+            for u in range(2):
+                wt_codes[t + u] = codes[:, u, :]
+                wt_plane[t + u] = plane[:, u, :]
+
+        def product(t, cols):
+            a_ps = psum.tile([P, cols.stop - cols.start], F32, name="a_ps%d_%d" % (t, cols.start))
+            nc.tensor.matmul_mx(out=a_ps[:], lhsT=wt_codes[t].bitcast(E2M1), lhsT_scale=wt_plane[t],
+                                rhs=xg_codes[:, cols].bitcast(E4M3), rhs_scale=xg_plane[:, cols], start=True, stop=True)
+            return a_ps
+
+        def put(t, cols):
+            nc.scalar.activation(out=boards[t][:].indirect(entries(idx2, cols)), in_=a_sb[t][:, cols], func=COPY)
+
+        def fetch(dst, lst, scale, t, cols):
+            nc.scalar.activation(out=dst[:, t, cols], in_=boards[t][:].indirect(entries(lst, cols)), func=COPY, scale=scale[:, t:t + 1])
+
+        def subtract(t, cols):
+            nc.vector.tensor_tensor(out=diff[:, t, cols], in0=first[:, t, cols], in1=second[:, t, cols], op=ALU.subtract)
+
+        def magnitude(t, cols):
+            pair = diff[:, t:t + 2, cols].rearrange("p t o -> p o t")
+            nc.vector.scalar_tensor_tensor(out=hid[:, cols, t:t + 2], in0=pair, scalar=-1.0, in1=pair, op0=ALU.mult, op1=ALU.max)
+
+        def fetch_both(t):
+            fetch(first, idx3, sa_t, t, places)
+            fetch(second, idx4, sb_t, t, places)
+            subtract(t, places)
+
+        def new_page(name, tag):
+            page = pool.tile([P, E], F32, name=name, tag=tag, align_bytes=64)
+            nc.vector.memset(page[:], 0.0)
+            return page
+
+        slots, slots_lo, slots_hi = slice(0, J), slice(0, J // 2), slice(J // 2, J)
+        places, places_lo, places_hi = slice(0, O), slice(0, O // 2), slice(O // 2, O)
         halves = N // P
-        page_a = [pool.tile([P, E], F32, name="page_a%d" % h, tag=("a_sb0", "board0")[h], align_bytes=64) for h in range(halves)]
-        page_b = [pool.tile([P, E], F32, name="page_b%d" % h, tag=("a_sb1", "board1")[h], align_bytes=64) for h in range(halves)]
-        for h in range(halves):
-            nc.vector.memset(page_a[h][:], 0.0)
-            nc.vector.memset(page_b[h][:], 0.0)
+
+        for q in range(4):
+            nc.vector.tensor_copy(out=w_plane[32 * q:32 * q + 4, :].bitcast(I32), in_=w_rows[:, q, :])
+        deal_pair(0)
+        nc.vector.tensor_copy(out=xg_codes[:], in_=xt_codes[:].indirect(idx[:]))
+        pick_scales(slots_lo)
+        nc.scalar.activation(out=a_sb[0][:, slots_lo], in_=product(0, slots_lo)[:], func=COPY)
+        put(0, slots_lo)
+        pick_scales(slots_hi)
+        nc.vector.tensor_copy(out=a_sb[1][:], in_=product(1, slots)[:])
+        put(1, slots)
+        nc.vector.tensor_copy(out=a_sb[0][:, slots_hi], in_=product(0, slots_hi)[:])
+        put(0, slots_hi)
+        deal_pair(2)
+        for t in (2, 3):
+            nc.vector.tensor_copy(out=a_sb[t][:], in_=product(t, slots)[:])
+        page_a = [new_page("page_a0", "a_sb0")]
+        page_b = [new_page("page_b0", "a_sb1")]
+        fetch_both(1)
+        put(2, slots)
+        fetch_both(0)
+        magnitude(0, places)
+        page_a.append(new_page("page_a1", "board0"))
+        page_b.append(new_page("page_b1", "board1"))
+        put(3, slots)
+        fetch_both(2)
+        fetch(first, idx3, sa_t, 3, places)
+        for cols in (places_lo, places_hi):
+            fetch(second, idx4, sb_t, 3, cols)
+            subtract(3, cols)
+        for cols in (places_lo, places_hi):
+            magnitude(2, cols)
+        for cols in (places_lo, places_hi):
+            nc.vector.quantize_mx(out=hid_codes[:, cols].bitcast(E4M3), scales=hid_plane[:, cols],
+                                  in_=hid[:, cols, :].rearrange("p o t -> p (o t)"))
 
         p_sb = []
         for h in range(halves):

@@ -88,7 +88,7 @@ def tile_list_ownboard_solo_one_pagetwice_kernel(tc, xt_words, xt_scales, w_word
         def deal_pair(t):
             codes = pool.tile([P, 2, P], U16, name="wt_codes%d" % t, tag="wt_codes", align_bytes=64)
             plane = pool.tile([P, 2, P], U8, name="wt_plane%d" % t, tag="wt_plane", align_bytes=64)
-            nc.vector.tensor_copy(out=codes[:], in_=w_codes[:].rearrange("p (m t) -> p t m", t=PACK)[:, t:t + 2, :])
+            (nc.scalar.copy if t == 0 else nc.vector.tensor_copy)(out=codes[:], in_=w_codes[:].rearrange("p (m t) -> p t m", t=PACK)[:, t:t + 2, :])
             nc.vector.tensor_copy(out=plane[:], in_=w_plane[:].rearrange("p (m t) -> p t m", t=PACK)[:, t:t + 2, :])
             for u in range(2):
                 wt_codes[t + u] = codes[:, u, :]
@@ -127,7 +127,7 @@ def tile_list_ownboard_solo_one_pagetwice_kernel(tc, xt_words, xt_scales, w_word
         places, places_lo, places_hi = slice(0, O), slice(0, O // 2), slice(O // 2, O)
         halves = N // P
 
-        for q in range(4):
+        for q in (1, 2, 3, 0):
             nc.vector.tensor_copy(out=w_plane[32 * q:32 * q + 4, :].bitcast(I32), in_=w_rows[:, q, :])
         deal_pair(0)
         nc.vector.tensor_copy(out=xg_codes[:], in_=xt_codes[:].indirect(idx[:]))
@@ -177,9 +177,7 @@ def tile_list_ownboard_solo_one_pagetwice_kernel(tc, xt_words, xt_scales, w_word
         for h in range(halves):
             nc.vector.tensor_copy(out=page_a[h][:].indirect(idx5[:]), in_=p_sb[h][:])
             nc.scalar.activation(out=page_b[h][:].indirect(idx6[:]), in_=p_sb[h][:], func=COPY)
-        for h in range(halves):
-            for s in range(2):
-                cols = slice(s * E // 2, (s + 1) * E // 2)
-                total = pool.tile([P, E // 2], F32, name="total%d_%d" % (h, s), align_bytes=64)
-                nc.vector.tensor_tensor(out=total[:], in0=page_a[h][:, cols], in1=page_b[h][:, cols], op=ALU.add)
-                nc.sync.dma_start(out=out[h * P:(h + 1) * P, cols], in_=total[:])
+        for h, lo, hi in ((0, 0, 512), (1, 0, 256), (1, 256, 512)):
+            total = pool.tile([P, hi - lo], F32, name="total%d_%d" % (h, lo), align_bytes=64)
+            nc.vector.tensor_tensor(out=total[:], in0=page_a[h][:, lo:hi], in1=page_b[h][:, lo:hi], op=ALU.add)
+            nc.sync.dma_start(out=out[h * P:(h + 1) * P, lo:hi], in_=total[:])

from contextlib import ExitStack

import concourse.mybir as mybir

K, T, J, R, C, O, N, E = 512, 1024, 256, 512, 512, 128, 256, 512
FLOPS = 2 * K * R * J + 2 * R * N * O

P = 128
PACK = 4
F32 = mybir.dt.float32
BF16 = mybir.dt.bfloat16
I32 = mybir.dt.int32
U32 = mybir.dt.uint32
U16 = mybir.dt.uint16
U8 = mybir.dt.uint8
E4M3 = mybir.dt.float8_e4m3fn_x4
E5M2 = mybir.dt.float8_e5m2_x4
E2M1 = mybir.dt.float4_e2m1fn_x4
ALU = mybir.AluOpType
COPY = mybir.ActivationFunctionType.Copy


def tile_list_ownboard_solo_one_pagetwice_kernel(tc, xt_words, xt_scales, w_words, w_scales, sa, sb, wb_words, wb_scales,
                                                    offs, offs2, offs3, offs4, offs5, offs6, out):
    nc = tc.nc
    with ExitStack() as ctx:
        lists = ctx.enter_context(tc.tile_pool(name="lists", bufs=1))
        pool = ctx.enter_context(tc.tile_pool(name="pool", bufs=1))
        psum = ctx.enter_context(tc.psum_pool(name="psum", bufs=1))

        def load_list(src, name):
            t = lists.tile(list(src.shape), U16, name=name)
            nc.sync.dma_start(out=t[:], in_=src)
            return t

        def load_plane(queue, plane, scales):
            for q in range(4):
                queue[q].dma_start(out=plane[32 * q:32 * q + 4, :].bitcast(I32), in_=scales[0, 4 * q:4 * q + 4, :].bitcast(I32))

        xt_plane = pool.tile([P, T], U8, name="xt_plane", align_bytes=64)
        w_plane = pool.tile([P, R], U8, name="w_plane", align_bytes=64)
        wb_plane = pool.tile([P, N], U8, name="wb_plane", align_bytes=64)
        nc.vector.memset(xt_plane[:].bitcast(I32), 0)
        nc.vector.memset(w_plane[:].bitcast(I32), 0)
        boards = [pool.tile([P, C], F32, name="board%d" % t, align_bytes=64) for t in range(PACK)]
        for t in range(PACK):
            (nc.vector if t == 0 else nc.gpsimd).memset(boards[t][:], 0.0)
        nc.vector.memset(wb_plane[:].bitcast(I32), 0)

        idx = load_list(offs, "idx")
        w_codes = pool.tile([P, R], U16, name="w_codes", align_bytes=64)
        nc.sync.dma_start(out=w_codes[:].bitcast(I32), in_=w_words[0].bitcast(I32))
        xt_codes = pool.tile([P, T], U32, name="xt_codes", align_bytes=64)
        nc.sync.dma_start(out=xt_codes[:].bitcast(I32), in_=xt_words[0].rearrange("p n t -> p (n t)").bitcast(I32))
        w_rows = pool.tile([4, 4, R // 4], I32, name="w_rows", align_bytes=64)
        nc.scalar.dma_start(out=w_rows[:], in_=w_scales[0].bitcast(I32).rearrange("(q r) c -> r q c", r=4))
        load_plane((nc.sync, nc.scalar, nc.sync, nc.scalar), xt_plane, xt_scales)
        idx2 = load_list(offs2, "idx2")
        sa_t = pool.tile([P, PACK], F32, name="sa_t")
        nc.sync.dma_start(out=sa_t[:], in_=sa.rearrange("(p t) o -> p (t o)", t=PACK))
        idx3 = load_list(offs3, "idx3")
        sb_t = pool.tile([P, PACK], F32, name="sb_t")
        nc.sync.dma_start(out=sb_t[:], in_=sb.rearrange("(p t) o -> p (t o)", t=PACK))
        idx4 = load_list(offs4, "idx4")
        wb_codes = pool.tile([P, N], U32, name="wb_codes", align_bytes=64)
        nc.sync.dma_start(out=wb_codes[:].bitcast(I32), in_=wb_words[0].rearrange("p n t -> p (n t)").bitcast(I32))
        load_plane([nc.sync] * 4, wb_plane, wb_scales)
        idx5 = load_list(offs5, "idx5")
        idx6 = load_list(offs6, "idx6")

        xg_plane = pool.tile([P, J], U8, name="xg_plane", align_bytes=64)
        xg_codes = pool.tile([P, J], U32, name="xg_codes", align_bytes=64)
        wt_codes, wt_plane = {}, {}
        a_sb = [pool.tile([P, J], F32, name="a_sb%d" % t, align_bytes=64) for t in range(PACK)]
        first = pool.tile([P, PACK, O], F32, name="first", align_bytes=64)
        second = pool.tile([P, PACK, O], F32, name="second", align_bytes=64)
        diff = pool.tile([P, PACK, O], F32, name="diff", align_bytes=64)
        hid = pool.tile([P, O, PACK], BF16, name="hid", align_bytes=64)
        hid_codes = pool.tile([P, O], U32, name="hid_codes", align_bytes=64)
        hid_plane = pool.tile([P, O], U8, name="hid_plane", align_bytes=64)

        def entries(lst, cols):
            return lst[:, cols.start // 16:cols.stop // 16]

        def pick_scales(cols):
            nc.vector.tensor_copy(out=xg_plane[:, cols], in_=xt_plane[:].indirect(entries(idx, cols)))

        def deal_pair(t):
            codes = pool.tile([P, 2, P], U16, name="wt_codes%d" % t, tag="wt_codes", align_bytes=64)
            plane = pool.tile([P, 2, P], U8, name="wt_plane%d" % t, tag="wt_plane", align_bytes=64)
            (nc.scalar.copy if t == 0 else nc.vector.tensor_copy)(out=codes[:], in_=w_codes[:].rearrange("p (m t) -> p t m", t=PACK)[:, t:t + 2, :])
            nc.vector.tensor_copy(out=plane[:], in_=w_plane[:].rearrange("p (m t) -> p t m", t=PACK)[:, t:t + 2, :])
            for u in range(2):
                wt_codes[t + u] = codes[:, u, :]
                wt_plane[t + u] = plane[:, u, :]

        def product(t, cols):
            a_ps = psum.tile([P, cols.stop - cols.start], F32, name="a_ps%d_%d" % (t, cols.start))
            nc.tensor.matmul_mx(out=a_ps[:], lhsT=wt_codes[t].bitcast(E2M1), lhsT_scale=wt_plane[t],
                                rhs=xg_codes[:, cols].bitcast(E4M3), rhs_scale=xg_plane[:, cols], start=True, stop=True)
            return a_ps

        def put(t, cols):
            nc.scalar.activation(out=boards[t][:].indirect(entries(idx2, cols)), in_=a_sb[t][:, cols], func=COPY)

        def fetch(dst, lst, scale, t, cols):
            nc.scalar.activation(out=dst[:, t, cols], in_=boards[t][:].indirect(entries(lst, cols)), func=COPY, scale=scale[:, t:t + 1])

        def subtract(t, cols):
            nc.vector.tensor_tensor(out=diff[:, t, cols], in0=first[:, t, cols], in1=second[:, t, cols], op=ALU.subtract)

        def magnitude(t, cols):
            pair = diff[:, t:t + 2, cols].rearrange("p t o -> p o t")
            nc.vector.scalar_tensor_tensor(out=hid[:, cols, t:t + 2], in0=pair, scalar=-1.0, in1=pair, op0=ALU.mult, op1=ALU.max)

        def fetch_both(t):
            fetch(first, idx3, sa_t, t, places)
            fetch(second, idx4, sb_t, t, places)
            subtract(t, places)

        def new_page(name, tag):
            page = pool.tile([P, E], F32, name=name, tag=tag, align_bytes=64)
            nc.vector.memset(page[:], 0.0)
            return page

        slots, slots_lo, slots_hi = slice(0, J), slice(0, J // 2), slice(J // 2, J)
        places, places_lo, places_hi = slice(0, O), slice(0, O // 2), slice(O // 2, O)
        halves = N // P

        for q in (1, 2, 3, 0):
            nc.vector.tensor_copy(out=w_plane[32 * q:32 * q + 4, :].bitcast(I32), in_=w_rows[:, q, :])
        deal_pair(0)
        nc.vector.tensor_copy(out=xg_codes[:], in_=xt_codes[:].indirect(idx[:]))
        pick_scales(slots_lo)
        nc.scalar.activation(out=a_sb[0][:, slots_lo], in_=product(0, slots_lo)[:], func=COPY)
        put(0, slots_lo)
        pick_scales(slots_hi)
        nc.vector.tensor_copy(out=a_sb[1][:], in_=product(1, slots)[:])
        put(1, slots)
        nc.vector.tensor_copy(out=a_sb[0][:, slots_hi], in_=product(0, slots_hi)[:])
        put(0, slots_hi)
        deal_pair(2)
        for t in (2, 3):
            nc.vector.tensor_copy(out=a_sb[t][:], in_=product(t, slots)[:])
        page_a = [new_page("page_a0", "a_sb0")]
        page_b = [new_page("page_b0", "a_sb1")]
        fetch_both(1)
        put(2, slots)
        fetch_both(0)
        magnitude(0, places)
        page_a.append(new_page("page_a1", "board0"))
        page_b.append(new_page("page_b1", "board1"))
        put(3, slots)
        fetch_both(2)
        fetch(first, idx3, sa_t, 3, places)
        for cols in (places_lo, places_hi):
            fetch(second, idx4, sb_t, 3, cols)
            subtract(3, cols)
        for cols in (places_lo, places_hi):
            magnitude(2, cols)
        for cols in (places_lo, places_hi):
            nc.vector.quantize_mx(out=hid_codes[:, cols].bitcast(E4M3), scales=hid_plane[:, cols],
                                  in_=hid[:, cols, :].rearrange("p o t -> p (o t)"))

        p_sb = []
        for h in range(halves):
            cols = slice(h * P, (h + 1) * P)
            p_ps = psum.tile([P, O], F32, name="p_ps%d" % h)
            nc.tensor.matmul_mx(out=p_ps[:], lhsT=wb_codes[:, cols].bitcast(E5M2), lhsT_scale=wb_plane[:, cols],
                                rhs=hid_codes[:].bitcast(E4M3), rhs_scale=hid_plane[:], start=True, stop=True)
            p_h = pool.tile([P, O], F32, name="p_sb%d" % h, align_bytes=64)
            if h == 0:
                nc.vector.tensor_copy(out=p_h[:], in_=p_ps[:])
            else:
                nc.scalar.copy(out=p_h[:], in_=p_ps[:])
            p_sb.append(p_h)
        for h in range(halves):
            nc.vector.tensor_copy(out=page_a[h][:].indirect(idx5[:]), in_=p_sb[h][:])
            nc.scalar.activation(out=page_b[h][:].indirect(idx6[:]), in_=p_sb[h][:], func=COPY)
        for h, lo, hi in ((0, 0, 512), (1, 0, 256), (1, 256, 512)):
            total = pool.tile([P, hi - lo], F32, name="total%d_%d" % (h, lo), align_bytes=64)
            nc.vector.tensor_tensor(out=total[:], in0=page_a[h][:, lo:hi], in1=page_b[h][:, lo:hi], op=ALU.add)
            nc.sync.dma_start(out=out[h * P:(h + 1) * P, lo:hi], in_=total[:])
